import numpy as np
import ml_dtypes


def mxq(x, axis, fmt="e4m3"):
    dtype, down = {"e4m3": (ml_dtypes.float8_e4m3fn, 7), "e5m2": (ml_dtypes.float8_e5m2, 14)}[fmt]
    v = np.moveaxis(np.asarray(x, np.float32).astype(ml_dtypes.bfloat16).astype(np.float64), axis, -1)
    blocks = v.reshape(v.shape[:-1] + (-1, 32))
    amax = np.abs(blocks).max(-1, keepdims=True)
    byte = np.maximum(np.where(amax > 0, np.frexp(amax)[1] - 1 + 127, 0) - down, 1)
    scale = np.exp2(byte - 127.0)
    codes = (blocks / scale).astype(np.float32).astype(dtype).astype(np.float64)
    return np.moveaxis((codes * scale).reshape(v.shape), -1, axis)


WIDE = False


def mx_kscale(k):
    if not WIDE:
        return np.ones(k)
    levels = np.array([10, -10, 5, -5, 0])
    if k % 512:
        return np.exp2(np.random.permutation(np.resize(levels, k // 32))).repeat(32)
    a = np.empty((k // 512, 16))
    for p in range(k // 512):
        a[p, :8] = np.random.permutation(np.resize(levels, 8))
        for g in range(8):
            far = levels[np.abs(levels - a[p, g]) >= 10]
            a[p, g + 8] = far[np.random.randint(len(far))]
    return np.exp2(a.ravel()).repeat(32)


def f64(x):
    return np.asarray(x).astype(np.float64)


def striped(idx):
    return np.tile(idx.reshape(-1, 16).T, (8, 1)).astype(np.uint16)


def unstriped(offs):
    return offs[:16].T.reshape(-1).astype(np.int64)


def striped8(idx):
    return np.concatenate([x.reshape(-1, 16).T for x in idx]).astype(np.uint16)


def runs(offs, k):
    lists = np.stack([offs[16 * r : 16 * r + 16].T.reshape(-1) for r in range(8)]).astype(np.int64)
    return lists[np.arange(k) % 512 // 64]


def pack_weight(w):
    k, n = w.shape
    w = f64(np.asarray(w, np.float32).astype(ml_dtypes.bfloat16)).reshape(k // 32, 32, n)
    amax = np.abs(w).max(1)
    byte = np.clip(np.where(amax > 0, np.frexp(amax)[1] - 1 + 127 - 7, 1), 1, 254)
    scaled = (w * np.exp2(127.0 - byte)[:, None, :]).reshape(k, n).astype(np.float32)
    words = np.ascontiguousarray(scaled.reshape(k // 512, 128, 4, n).transpose(0, 1, 3, 2)).astype(ml_dtypes.float8_e4m3fn).view(np.uint8)
    return words, np.ascontiguousarray(byte.astype(np.uint8).reshape(k // 512, 16, n))


def unpack_weight(words, scales):
    g, p, n, _ = words.shape
    vals = np.ascontiguousarray(words).view(ml_dtypes.float8_e4m3fn).astype(np.float64) * np.repeat(np.exp2(scales.astype(np.float64) - 127.0), 8, axis=1)[..., None]
    return vals.transpose(0, 1, 3, 2).reshape(g * 512, n)


E2M1 = np.array([0.0, 0.5, 1.0, 1.5, 2.0, 3.0, 4.0, 6.0, -0.0, -0.5, -1.0, -1.5, -2.0, -3.0, -4.0, -6.0])


def pack_fp4(w):
    k, n = w.shape
    w = f64(np.asarray(w, np.float32).astype(ml_dtypes.bfloat16)).reshape(k // 32, 32, n)
    amax = np.abs(w).max(1)
    mant, ex = np.frexp(amax / 6.0)
    byte = np.clip(np.where(amax > 0, np.where(mant > 0.5, ex, ex - 1) + 127, 1), 1, 254)
    scaled = (w * np.exp2(127.0 - byte)[:, None, :]).reshape(k, n).astype(np.float32)
    c = np.ascontiguousarray(scaled.reshape(k // 512, 128, 4, n).transpose(0, 1, 3, 2)).astype(ml_dtypes.float4_e2m1fn).view(np.uint8) & 0xF
    words = (c[..., 0::2] | (c[..., 1::2] << 4)).reshape(k // 512, 128, 2 * n)
    return np.ascontiguousarray(words), np.ascontiguousarray(byte.astype(np.uint8).reshape(k // 512, 16, n))


def unpack_fp4(words, scales):
    g, _, n = scales.shape
    words = np.ascontiguousarray(words).reshape(g, 128, n, 2)
    nib = np.empty((g, 128, n, 4), np.uint8)
    nib[..., 0::2] = words & 0xF
    nib[..., 1::2] = words >> 4
    vals = E2M1[nib] * np.repeat(np.exp2(scales.astype(np.float64) - 127.0), 8, axis=1)[..., None]
    return vals.transpose(0, 1, 3, 2).reshape(g * 512, n)


def relu(v):
    return np.maximum(v, 0.0)

def planes(y):
    n, m = y.shape
    v = y.astype(np.float32).astype(ml_dtypes.bfloat16).astype(np.float64).reshape(n // 32, 32, m)
    top = np.abs(v).max(1)
    byte = np.clip(np.where(top > 0, np.frexp(top)[1] - 1 + 127 - 7, 1), 1, 254)
    codes = (v * np.exp2(127.0 - byte)[:, None, :]).reshape(n, m).astype(np.float32).astype(ml_dtypes.float8_e4m3fn).view(np.uint8)
    words = codes.reshape(n // 512, 128, 4, m).transpose(0, 1, 3, 2)
    return np.ascontiguousarray(words), np.ascontiguousarray(byte.astype(np.uint8).reshape(n // 512, 16, m))


K, T, S, N, H = 512, 2048, 512, 512, 512


def setup_inputs():
    n = np.random.standard_normal
    s = mx_kscale(K)[:, None]
    u = mx_kscale(H)
    packed_xT = pack_weight(n((K, T)) * s)
    packed_w1 = pack_fp4(n((K, H)) / np.sqrt(K) / s)
    packed_w2 = pack_fp4(n((H, N)) / np.sqrt(H) / u[:, None])
    packed_w3 = pack_fp4(n((H, N)) / np.sqrt(H) / u[:, None])
    return {
        "x_words": packed_xT[0],
        "x_scales": packed_xT[1],
        "w1_words": packed_w1[0],
        "w1_scales": packed_w1[1],
        "gn": (np.random.uniform(0.5, 1.5, (H, 1)) * u[:, None]).astype(np.float32),
        "w2_words": packed_w2[0],
        "w2_scales": packed_w2[1],
        "gm": (np.random.uniform(0.5, 1.5, (H, 1)) * u[:, None]).astype(np.float32),
        "w3_words": packed_w3[0],
        "w3_scales": packed_w3[1],
        "offs": striped(np.random.permutation(T)[:S]),
        "n1": striped8(np.stack([np.random.permutation(S) for _ in range(8)])),
        "n2": striped8(np.stack([np.random.permutation(S) for _ in range(8)])),
        "n3": striped8(np.stack([np.random.permutation(S) for _ in range(8)])),
        "n4": striped8(np.stack([np.random.permutation(S) for _ in range(8)])),
        "n5": striped8(np.stack([np.random.permutation(S) for _ in range(8)])),
    }


def reference(x_words, x_scales, w1_words, w1_scales, gn, w2_words, w2_scales, gm, w3_words, w3_scales, offs, n1, n2, n3, n4, n5):
    xq = unpack_weight(x_words, x_scales)[:, unstriped(offs)]
    y = unpack_fp4(w1_words, w1_scales).T @ xq
    rl = relu(y)
    ds = np.zeros((H, S))
    ds[np.arange(H)[:, None], runs(n1, H)] = rl
    z = f64(gn) * (ds - (0.5 * y))
    a = unpack_fp4(w2_words, w2_scales).T @ mxq(z, 0, "e4m3")
    z2 = f64(gm) * (y[np.arange(H)[:, None], runs(n2, H)] - (y[np.arange(H)[:, None], runs(n3, H)]))
    b = unpack_fp4(w3_words, w3_scales).T @ mxq(z2, 0, "e4m3")
    out_0 = 0.75 * (a * (b[np.arange(N)[:, None], runs(n5, N)]) - ((a[np.arange(N)[:, None], runs(n4, N)]) * b))
    return (out_0,) + planes(out_0)

@@ -1,0 +1,269 @@
+from contextlib import ExitStack
+
+import concourse.mybir as mybir
+from concourse.masks import make_identity
+
+F32 = mybir.dt.float32
+BF16 = mybir.dt.bfloat16
+I32 = mybir.dt.int32
+U32 = mybir.dt.uint32
+U16 = mybir.dt.uint16
+U8 = mybir.dt.uint8
+FP8X4 = mybir.dt.float8_e4m3fn_x4
+FP4X4 = mybir.dt.float4_e2m1fn_x4
+ALU = mybir.AluOpType
+ACT = mybir.ActivationFunctionType
+
+P = 128
+T = 2048
+S = 512
+D = 512
+PACK = 4
+CHUNKS = ((0, 256), (256, 128), (384, 128))
+
+FLOPS = 3 * 2 * D * D * S
+
+
+def tile_picked_forkcrossbsendgap_none_po_kernel(
+    tc, x_words, x_scales, w1_words, w1_scales, gn, w2_words, w2_scales, gm, w3_words, w3_scales,
+    offs, n1, n2, n3, n4, n5, out_0, out_1, out_2,
+):
+    nc = tc.nc
+    with ExitStack() as ctx:
+        lists = ctx.enter_context(tc.tile_pool(name="lists", bufs=1))
+        sb = ctx.enter_context(tc.tile_pool(name="sb", bufs=1))
+        ps = ctx.enter_context(tc.psum_pool(name="ps", bufs=1))
+
+        def sbuf(shape, dtype, name, tag=None):
+            return sb.tile(shape, dtype, name=name, tag=tag or name, align_bytes=64)
+
+        def bank(name, tag):
+            return ps.tile([P, 512], F32, name=name, tag=tag)
+
+        def load_list(src, name):
+            t = lists.tile([P, S // 16], U16, name=name)
+            nc.sync.dma_start(t[:], src)
+            return t
+
+        def load_scale_rows(queue, dst, src):
+            for q in range(4):
+                queue.dma_start(dst[32 * q : 32 * q + 4, :].bitcast(I32), src[0, 4 * q : 4 * q + 4, :].bitcast(I32))
+
+        def cleared(width, name, eng):
+            t = sbuf([P, width], U8, name)
+            eng.memset(t[:].bitcast(I32), 0)
+            return t
+
+        def load_words(queue, src, name):
+            t = sbuf([P, 2 * D], U8, name)
+            queue.dma_start(t[:].bitcast(I32), src[0].bitcast(I32))
+            return t
+
+        def deal_words(raw, name):
+            t = sbuf([P, 2 * D], U8, name)
+            nc.vector.tensor_copy(
+                t[:].rearrange("p (t m b) -> p t m b", t=PACK, b=2), raw[:].rearrange("p (m t b) -> p t m b", t=PACK, b=2)
+            )
+            return t
+
+        def deal_scales(raw, name):
+            t = sbuf([P, D], U8, name)
+            nc.vector.tensor_copy(t[:].rearrange("p (t m) -> p t m", t=PACK), raw[:].rearrange("p (m t) -> p t m", t=PACK))
+            return t
+
+        def product(out, words, scales, t, codes, code_scales):
+            nc.tensor.matmul_mx(
+                out=out,
+                lhsT=words[:, 2 * P * t : 2 * P * (t + 1)].bitcast(FP4X4),
+                lhsT_scale=scales[:, P * t : P * (t + 1)],
+                rhs=codes.bitcast(FP8X4),
+                rhs_scale=code_scales,
+                start=True,
+                stop=True,
+            )
+
+        def interleave(copy, dst, src):
+            copy(dst[:].rearrange("p (c i t) -> p c t i", i=4, t=PACK), src[:].rearrange("p t (c i) -> p c t i", i=4))
+
+        xs = cleared(T, "xs", nc.vector)
+        w1s_raw = cleared(D, "w1s_raw", nc.vector)
+        w2s_raw = cleared(D, "w2s_raw", nc.gpsimd)
+        w3s_raw = cleared(D, "w3s_raw", nc.gpsimd)
+        offs_t = load_list(offs, "offs_t")
+        w1_raw = load_words(nc.scalar, w1_words, "w1_raw")
+        xw = sbuf([P, T], U32, "xw")
+        nc.sync.dma_start(xw[:].bitcast(I32), x_words[0].rearrange("p n t -> p (n t)").bitcast(I32))
+        load_scale_rows(nc.scalar, xs, x_scales)
+        load_scale_rows(nc.scalar, w1s_raw, w1_scales)
+        gn_t = sbuf([P, PACK], F32, "gn_t")
+        nc.sync.dma_start(gn_t[:], gn.rearrange("(p t) o -> p (t o)", t=PACK))
+        n1_t = load_list(n1, "n1_t")
+        gm_t = sbuf([P, PACK], F32, "gm_t")
+        nc.sync.dma_start(gm_t[:], gm.rearrange("(p t) o -> p (t o)", t=PACK))
+        w2_raw = load_words(nc.sync, w2_words, "w2_raw")
+        load_scale_rows(nc.sync, w2s_raw, w2_scales)
+        w3_raw = load_words(nc.sync, w3_words, "w3_raw")
+        load_scale_rows(nc.sync, w3s_raw, w3_scales)
+        n3_t = load_list(n3, "n3_t")
+        n2_t = load_list(n2, "n2_t")
+        n4_t = load_list(n4, "n4_t")
+        n5_t = load_list(n5, "n5_t")
+        ident = sbuf([P, P], F32, "ident")
+        make_identity(nc, ident[:])
+        half_gn = sbuf([P, PACK], F32, "half_gn")
+        nc.scalar.activation(half_gn[:], gn_t[:], ACT.Copy, scale=-0.5)
+
+        w1 = deal_words(w1_raw, "w1")
+        xq_s = sbuf([P, S], U8, "xq_s")
+        nc.vector.tensor_copy(xq_s[:], xs[:].indirect(offs_t[:]))
+        w1s = deal_scales(w1s_raw, "w1s")
+        xq = sbuf([P, S], U32, "xq")
+        nc.vector.tensor_copy(xq[:], xw[:].indirect(offs_t[:]))
+        y = [bank(f"y{t}", f"acc{t}") for t in range(PACK)]
+        for t in range(PACK):
+            product(y[t][:], w1, w1s, t, xq[:], xq_s[:])
+        w2 = deal_words(w2_raw, "w2")
+
+        sent = [sbuf([P, S], F32, f"sent{t}") for t in range(PACK)]
+        nc.vector.tensor_scalar(sent[0][:], y[0][:], 0.0, gn_t[:, 0:1], ALU.max, ALU.mult)
+        for t in range(1, PACK):
+            pos = sbuf([P, S], F32, f"pos{t}")
+            nc.scalar.activation(pos[:], y[t][:], ACT.Relu)
+            nc.scalar.activation(sent[t][:], pos[:], ACT.Copy, scale=gn_t[:, t : t + 1])
+        ds = [sbuf([P, 2 * S], F32, f"ds{t}") for t in range(PACK)]
+        for t in range(PACK):
+            nc.vector.tensor_copy(ds[t][:].indirect(n1_t[:]), sent[t][:])
+        less = [sbuf([P, S], F32, f"less{t}") for t in range(PACK)]
+        for t in range(PACK):
+            nc.scalar.activation(less[t][:], y[t][:], ACT.Copy, scale=half_gn[:, t : t + 1])
+        ym = [sbuf([P, S], F32, f"ym{t}") for t in range(PACK)]
+        for t in range(PACK):
+            nc.scalar.activation(ym[t][:], y[t][:], ACT.Copy, scale=gm_t[:, t : t + 1])
+        w2s = deal_scales(w2s_raw, "w2s")
+        w3 = deal_words(w3_raw, "w3")
+        w3s = deal_scales(w3s_raw, "w3s")
+
+        back = [bank(f"back{h}", f"back{h}") for h in range(2)]
+        for u in range(2):
+            turned = [bank(f"turned{u}{h}", f"turned{h}") for h in range(2)]
+            for e in range(2):
+                t = 2 * u + e
+                for h in range(2):
+                    for c in range(2):
+                        cols = slice(256 * h + P * c, 256 * h + P * (c + 1))
+                        dst = turned[h][:, P * (2 * c + e) : P * (2 * c + e + 1)]
+                        nc.tensor.matmul(dst, less[t][:, cols], ident[:], start=True, stop=False, is_transpose=True)
+                        nc.tensor.matmul(dst, ds[t][:, cols], ident[:], start=False, stop=True, is_transpose=True)
+            for h in range(2):
+                pairs = sbuf([P, 512], BF16, f"pairs{u}{h}")
+                nc.scalar.copy(
+                    pairs[:].rearrange("j (c p e) -> j c p e", c=2, e=2), turned[h][:].rearrange("j (c e p) -> j c p e", c=2, e=2)
+                )
+                for c in range(2):
+                    nc.tensor.transpose(
+                        back[h][:, 256 * u + P * c : 256 * u + P * (c + 1)],
+                        pairs[:].bitcast(F32)[:, P * c : P * (c + 1)],
+                        ident[:],
+                    )
+        z_in = sbuf([P, PACK * S], BF16, "z_in")
+        for h in range(2):
+            nc.scalar.copy(
+                z_in[:].bitcast(F32)[:, 512 * h : 512 * (h + 1)].rearrange("p (j u) -> p j u", u=2),
+                back[h][:].rearrange("p (u j) -> p j u", u=2),
+            )
+
+        def gap(k, reuse):
+            c0, w = CHUNKS[k]
+            cut = slice(c0 // 16, (c0 + w) // 16)
+            second = sbuf([P, PACK, w], F32, f"second{k}", tag=reuse)
+            for t in range(PACK):
+                nc.vector.tensor_copy(second[:, t, :], ym[t][:].indirect(n3_t[:, cut]))
+            diff = sbuf([P, PACK, w], F32, f"diff{k}")
+            for t in range(PACK):
+                nc.vector.tensor_tensor(diff[:, t, :], ym[t][:].indirect(n2_t[:, cut]), second[:, t, :], ALU.subtract)
+            return diff
+
+        def round_gap(k, diff):
+            w = CHUNKS[k][1]
+            z2_in = sbuf([P, PACK * w], BF16, f"z2_in{k}")
+            interleave(nc.scalar.copy, z2_in, diff)
+            return z2_in
+
+        z2_codes = sbuf([P, S], U32, "z2_codes")
+        z2_scales = sbuf([P, S], U8, "z2_scales")
+        b = [sbuf([P, S], F32, f"b{t}") for t in range(PACK)]
+        b_tags = (("turned0", "turned1"), ("back0",), ("back1",))
+
+        def third(k, z2_in):
+            c0, w = CHUNKS[k]
+            cols = slice(c0, c0 + w)
+            nc.vector.quantize_mx(out=z2_codes[:, cols].bitcast(FP8X4), scales=z2_scales[:, cols], in_=z2_in[:])
+            banks = [bank(f"bacc{k}{i}", tag) for i, tag in enumerate(b_tags[k])]
+            per = 512 // w
+            places = [banks[t // per][:, w * (t % per) : w * (t % per + 1)] for t in range(PACK)]
+            for t in range(PACK):
+                product(places[t], w3, w3s, t, z2_codes[:, cols], z2_scales[:, cols])
+            return places
+
+        def drain_b(k, places):
+            c0, w = CHUNKS[k]
+            for t in range(PACK):
+                nc.scalar.copy(b[t][:, c0 : c0 + w], places[t])
+
+        diff0 = gap(0, "sent3")
+        z_codes = sbuf([P, S], U32, "z_codes")
+        z_scales = sbuf([P, S], U8, "z_scales")
+        nc.vector.quantize_mx(out=z_codes[:].bitcast(FP8X4), scales=z_scales[:], in_=z_in[:])
+        acc = [bank(f"a{t}", f"acc{t}") for t in range(PACK)]
+        for t in range(PACK):
+            product(acc[t][:], w2, w2s, t, z_codes[:], z_scales[:])
+        z2_in0 = round_gap(0, diff0)
+        a = [sbuf([P, S], F32, f"a{t}") for t in range(PACK)]
+        for t in range(PACK):
+            nc.scalar.activation(a[t][:], acc[t][:], ACT.Copy, scale=0.75)
+        diff1 = gap(1, "z_in")
+        places0 = third(0, z2_in0)
+        diff2 = gap(2, "z2_in0")
+        z2_in1 = round_gap(1, diff1)
+        drain_b(0, places0)
+        places1 = third(1, z2_in1)
+        z2_in2 = round_gap(2, diff2)
+        drain_b(1, places1)
+
+        def cross(k, name, window, plain, offsets):
+            c0, w = CHUNKS[k]
+            res = sbuf([P, PACK, w], F32, f"{name}{k}")
+            for t in range(PACK):
+                nc.vector.tensor_tensor(
+                    res[:, t, :], window[t][:].indirect(offsets[:, c0 // 16 : (c0 + w) // 16]), plain[t][:, c0 : c0 + w], ALU.mult
+                )
+            return res
+
+        minus = [cross(0, "minus", a, b, n4_t)]
+        places2 = third(2, z2_in2)
+        drain_b(2, places2)
+        minus.append(cross(1, "minus", a, b, n4_t))
+
+        o_codes = sbuf([P, S], U32, "o_codes")
+        o_scales = sbuf([P, S], U8, "o_scales")
+        rows = out_0.rearrange("(p t) j -> p t j", t=PACK)
+        words_out = out_1[0].rearrange("p n t -> p (n t)").bitcast(I32)
+        last = len(CHUNKS) - 1
+        rounded = []
+        for k, (c0, w) in enumerate(CHUNKS):
+            if k == last:
+                minus.append(cross(k, "minus", a, b, n4_t))
+            plus = cross(k, "plus", b, a, n5_t)
+            res = sbuf([P, PACK, w], F32, f"res{k}")
+            nc.vector.tensor_tensor(res[:], plus[:], minus[k][:], ALU.subtract)
+            nc.sync.dma_start(rows[:, :, c0 : c0 + w], res[:])
+            o_in = sbuf([P, PACK * w], BF16, f"o_in{k}")
+            interleave(nc.vector.tensor_copy if k == last else nc.scalar.copy, o_in, res)
+            rounded.append(o_in)
+        for k, (c0, w) in enumerate(CHUNKS):
+            cols = slice(c0, c0 + w)
+            nc.vector.quantize_mx(out=o_codes[:, cols].bitcast(FP8X4), scales=o_scales[:, cols], in_=rounded[k][:])
+            nc.sync.dma_start(words_out[:, cols], o_codes[:, cols].bitcast(I32))
+        for q in range(4):
+            queue = nc.scalar if q % 2 == 0 else nc.sync
+            queue.dma_start(out_2[0, 4 * q : 4 * q + 4, :].bitcast(I32), o_scales[32 * q : 32 * q + 4, :].bitcast(I32))

@@ -45,8 +45,8 @@ def tile_picked_forkcrossbsendgap_none_po_kernel(
             nc.sync.dma_start(t[:], src)
             return t
 
-        def load_scale_rows(queue, dst, src):
-            for q in range(4):
+        def load_scale_rows(queues, dst, src):
+            for q, queue in enumerate(queues):
                 queue.dma_start(dst[32 * q : 32 * q + 4, :].bitcast(I32), src[0, 4 * q : 4 * q + 4, :].bitcast(I32))
 
         def cleared(width, name, eng):
@@ -54,21 +54,22 @@ def tile_picked_forkcrossbsendgap_none_po_kernel(
             eng.memset(t[:].bitcast(I32), 0)
             return t
 
-        def load_words(queue, src, name):
-            t = sbuf([P, 2 * D], U8, name)
-            queue.dma_start(t[:].bitcast(I32), src[0].bitcast(I32))
-            return t
+        def load_words(dst, src):
+            nc.sync.dma_start(dst.bitcast(I32), src[0].bitcast(I32))
 
-        def deal_words(raw, name):
+        def deal_words(eng, raw, name):
             t = sbuf([P, 2 * D], U8, name)
-            nc.vector.tensor_copy(
-                t[:].rearrange("p (t m b) -> p t m b", t=PACK, b=2), raw[:].rearrange("p (m t b) -> p t m b", t=PACK, b=2)
+            eng.tensor_copy(
+                t[:].rearrange("p (t m b) -> p t m b", t=PACK, b=2), raw.rearrange("p (m t b) -> p t m b", t=PACK, b=2)
             )
             return t
 
-        def deal_scales(raw, name):
+        def deal_scales(eng, raw, name, cuts=((0, PACK),)):
             t = sbuf([P, D], U8, name)
-            nc.vector.tensor_copy(t[:].rearrange("p (t m) -> p t m", t=PACK), raw[:].rearrange("p (m t) -> p t m", t=PACK))
+            for lo, hi in cuts:
+                eng.tensor_copy(
+                    t[:].rearrange("p (t m) -> p t m", t=PACK)[:, lo:hi, :], raw[:].rearrange("p (m t) -> p t m", t=PACK)[:, lo:hi, :]
+                )
             return t
 
         def product(out, words, scales, t, codes, code_scales):
@@ -86,24 +87,19 @@ def tile_picked_forkcrossbsendgap_none_po_kernel(
             copy(dst[:].rearrange("p (c i t) -> p c t i", i=4, t=PACK), src[:].rearrange("p t (c i) -> p c t i", i=4))
 
         xs = cleared(T, "xs", nc.vector)
-        w1s_raw = cleared(D, "w1s_raw", nc.vector)
-        w2s_raw = cleared(D, "w2s_raw", nc.gpsimd)
-        w3s_raw = cleared(D, "w3s_raw", nc.gpsimd)
+        ws_raw = cleared(D, "ws_raw", nc.gpsimd)
         offs_t = load_list(offs, "offs_t")
-        w1_raw = load_words(nc.scalar, w1_words, "w1_raw")
-        xw = sbuf([P, T], U32, "xw")
-        nc.sync.dma_start(xw[:].bitcast(I32), x_words[0].rearrange("p n t -> p (n t)").bitcast(I32))
-        load_scale_rows(nc.scalar, xs, x_scales)
-        load_scale_rows(nc.scalar, w1s_raw, w1_scales)
+        w1_raw = sbuf([P, 2 * D], U8, "w1_raw")
+        load_words(w1_raw[:], w1_words)
         gn_t = sbuf([P, PACK], F32, "gn_t")
         nc.sync.dma_start(gn_t[:], gn.rearrange("(p t) o -> p (t o)", t=PACK))
+        xw = sbuf([P, T], U32, "xw")
+        nc.sync.dma_start(xw[:].bitcast(I32), x_words[0].rearrange("p n t -> p (n t)").bitcast(I32))
+        load_scale_rows((nc.scalar,) * 4, ws_raw, w1_scales)
+        load_scale_rows((nc.sync,) * 4, xs, x_scales)
         n1_t = load_list(n1, "n1_t")
         gm_t = sbuf([P, PACK], F32, "gm_t")
         nc.sync.dma_start(gm_t[:], gm.rearrange("(p t) o -> p (t o)", t=PACK))
-        w2_raw = load_words(nc.sync, w2_words, "w2_raw")
-        load_scale_rows(nc.sync, w2s_raw, w2_scales)
-        w3_raw = load_words(nc.sync, w3_words, "w3_raw")
-        load_scale_rows(nc.sync, w3s_raw, w3_scales)
         n3_t = load_list(n3, "n3_t")
         n2_t = load_list(n2, "n2_t")
         n4_t = load_list(n4, "n4_t")
@@ -113,16 +109,24 @@ def tile_picked_forkcrossbsendgap_none_po_kernel(
         half_gn = sbuf([P, PACK], F32, "half_gn")
         nc.scalar.activation(half_gn[:], gn_t[:], ACT.Copy, scale=-0.5)
 
-        w1 = deal_words(w1_raw, "w1")
-        xq_s = sbuf([P, S], U8, "xq_s")
-        nc.vector.tensor_copy(xq_s[:], xs[:].indirect(offs_t[:]))
-        w1s = deal_scales(w1s_raw, "w1s")
+        w1 = deal_words(nc.vector, w1_raw[:], "w1")
+        w1s = deal_scales(nc.vector, ws_raw, "w1s")
         xq = sbuf([P, S], U32, "xq")
         nc.vector.tensor_copy(xq[:], xw[:].indirect(offs_t[:]))
+        xq_s = sbuf([P, S], U8, "xq_s", tag="xw")
+        nc.vector.tensor_copy(xq_s[:], xs[:].indirect(offs_t[:]))
         y = [bank(f"y{t}", f"acc{t}") for t in range(PACK)]
         for t in range(PACK):
             product(y[t][:], w1, w1s, t, xq[:], xq_s[:])
-        w2 = deal_words(w2_raw, "w2")
+        w_raw = sbuf([P, 2, 2 * D], U8, "w_raw", tag="xs")
+        load_words(w_raw[:, 0, :], w2_words)
+        load_words(w_raw[:, 1, :], w3_words)
+        load_scale_rows((nc.sync,) * 4, ws_raw, w2_scales)
+        w2s = deal_scales(nc.gpsimd, ws_raw, "w2s")
+        load_scale_rows((nc.sync,) * 4, ws_raw, w3_scales)
+        w2 = deal_words(nc.gpsimd, w_raw[:, 0, :], "w2")
+        w3s = deal_scales(nc.gpsimd, ws_raw, "w3s")
+        w3 = deal_words(nc.gpsimd, w_raw[:, 1, :], "w3")
 
         sent = [sbuf([P, S], F32, f"sent{t}") for t in range(PACK)]
         nc.vector.tensor_scalar(sent[0][:], y[0][:], 0.0, gn_t[:, 0:1], ALU.max, ALU.mult)
@@ -139,9 +143,6 @@ def tile_picked_forkcrossbsendgap_none_po_kernel(
         ym = [sbuf([P, S], F32, f"ym{t}") for t in range(PACK)]
         for t in range(PACK):
             nc.scalar.activation(ym[t][:], y[t][:], ACT.Copy, scale=gm_t[:, t : t + 1])
-        w2s = deal_scales(w2s_raw, "w2s")
-        w3 = deal_words(w3_raw, "w3")
-        w3s = deal_scales(w3s_raw, "w3s")
 
         back = [bank(f"back{h}", f"back{h}") for h in range(2)]
         for u in range(2):
@@ -172,20 +173,25 @@ def tile_picked_forkcrossbsendgap_none_po_kernel(
                 back[h][:].rearrange("p (u j) -> p j u", u=2),
             )
 
-        def gap(k, reuse):
+        def fetch(h, reuse):
+            second = sbuf([P, PACK, 256], F32, f"second{h}", tag=reuse)
+            for t in range(PACK):
+                nc.vector.tensor_copy(second[:, t, :], ym[t][:].indirect(n3_t[:, 16 * h : 16 * (h + 1)]))
+            return second
+
+        def gap(k, second, reuse=None):
             c0, w = CHUNKS[k]
             cut = slice(c0 // 16, (c0 + w) // 16)
-            second = sbuf([P, PACK, w], F32, f"second{k}", tag=reuse)
+            diff = sbuf([P, PACK, w], F32, f"diff{k}", tag=reuse)
             for t in range(PACK):
-                nc.vector.tensor_copy(second[:, t, :], ym[t][:].indirect(n3_t[:, cut]))
-            diff = sbuf([P, PACK, w], F32, f"diff{k}")
-            for t in range(PACK):
-                nc.vector.tensor_tensor(diff[:, t, :], ym[t][:].indirect(n2_t[:, cut]), second[:, t, :], ALU.subtract)
+                nc.vector.tensor_tensor(
+                    diff[:, t, :], ym[t][:].indirect(n2_t[:, cut]), second[:, t, c0 % 256 : c0 % 256 + w], ALU.subtract
+                )
             return diff
 
-        def round_gap(k, diff):
+        def round_gap(k, diff, reuse=None):
             w = CHUNKS[k][1]
-            z2_in = sbuf([P, PACK * w], BF16, f"z2_in{k}")
+            z2_in = sbuf([P, PACK * w], BF16, f"z2_in{k}", tag=reuse)
             interleave(nc.scalar.copy, z2_in, diff)
             return z2_in
 
@@ -210,39 +216,39 @@ def tile_picked_forkcrossbsendgap_none_po_kernel(
             for t in range(PACK):
                 nc.scalar.copy(b[t][:, c0 : c0 + w], places[t])
 
-        diff0 = gap(0, "sent3")
+        diff0 = gap(0, fetch(0, "sent3"))
         z_codes = sbuf([P, S], U32, "z_codes")
         z_scales = sbuf([P, S], U8, "z_scales")
         nc.vector.quantize_mx(out=z_codes[:].bitcast(FP8X4), scales=z_scales[:], in_=z_in[:])
         acc = [bank(f"a{t}", f"acc{t}") for t in range(PACK)]
         for t in range(PACK):
             product(acc[t][:], w2, w2s, t, z_codes[:], z_scales[:])
-        z2_in0 = round_gap(0, diff0)
+        z2_in0 = round_gap(0, diff0, "pairs11")
         a = [sbuf([P, S], F32, f"a{t}") for t in range(PACK)]
         for t in range(PACK):
             nc.scalar.activation(a[t][:], acc[t][:], ACT.Copy, scale=0.75)
-        diff1 = gap(1, "z_in")
+        second1 = fetch(1, "z_in")
+        diff1 = gap(1, second1)
         places0 = third(0, z2_in0)
-        diff2 = gap(2, "z2_in0")
+        diff2 = gap(2, second1, "pairs11")
         z2_in1 = round_gap(1, diff1)
         drain_b(0, places0)
         places1 = third(1, z2_in1)
         z2_in2 = round_gap(2, diff2)
         drain_b(1, places1)
 
-        def cross(k, name, window, plain, offsets):
-            c0, w = CHUNKS[k]
-            res = sbuf([P, PACK, w], F32, f"{name}{k}")
+        def cross(c0, w, name, window, plain, offsets):
+            res = sbuf([P, PACK, w], F32, f"{name}{c0}")
             for t in range(PACK):
                 nc.vector.tensor_tensor(
                     res[:, t, :], window[t][:].indirect(offsets[:, c0 // 16 : (c0 + w) // 16]), plain[t][:, c0 : c0 + w], ALU.mult
                 )
             return res
 
-        minus = [cross(0, "minus", a, b, n4_t)]
+        minus = [cross(0, 256, "minus", a, b, n4_t)]
         places2 = third(2, z2_in2)
         drain_b(2, places2)
-        minus.append(cross(1, "minus", a, b, n4_t))
+        minus.append(cross(256, 128, "minus", a, b, n4_t))
 
         o_codes = sbuf([P, S], U32, "o_codes")
         o_scales = sbuf([P, S], U8, "o_scales")
@@ -252,8 +258,8 @@ def tile_picked_forkcrossbsendgap_none_po_kernel(
         rounded = []
         for k, (c0, w) in enumerate(CHUNKS):
             if k == last:
-                minus.append(cross(k, "minus", a, b, n4_t))
-            plus = cross(k, "plus", b, a, n5_t)
+                minus.append(cross(c0, w, "minus", a, b, n4_t))
+            plus = cross(c0, w, "plus", b, a, n5_t)
             res = sbuf([P, PACK, w], F32, f"res{k}")
             nc.vector.tensor_tensor(res[:], plus[:], minus[k][:], ALU.subtract)
             nc.sync.dma_start(rows[:, :, c0 : c0 + w], res[:])

@@ -19,6 +19,11 @@ T = 2048
 S = 512
 D = 512
 PACK = 4
+BANK = 512
+HALF = S // 2
+GROUP = 16
+QUADRANTS = 4
+LINE = 4
 CHUNKS = ((0, 256), (256, 128), (384, 128))
 
 FLOPS = 3 * 2 * D * D * S
@@ -38,39 +43,44 @@ def tile_picked_forkcrossbsendgap_none_po_kernel(
             return sb.tile(shape, dtype, name=name, tag=tag or name, align_bytes=64)
 
         def bank(name, tag):
-            return ps.tile([P, 512], F32, name=name, tag=tag)
+            return ps.tile([P, BANK], F32, name=name, tag=tag)
 
         def load_list(src, name):
-            t = lists.tile([P, S // 16], U16, name=name)
-            nc.sync.dma_start(t[:], src)
-            return t
+            held = lists.tile([P, S // GROUP], U16, name=name)
+            nc.sync.dma_start(held[:], src)
+            return held
 
-        def load_scale_rows(queues, dst, src):
-            for q, queue in enumerate(queues):
+        def entries(held, first, count):
+            return held[:, first // GROUP : (first + count) // GROUP]
+
+        def load_scale_rows(queue, dst, src):
+            for q in range(QUADRANTS):
                 queue.dma_start(dst[32 * q : 32 * q + 4, :].bitcast(I32), src[0, 4 * q : 4 * q + 4, :].bitcast(I32))
 
-        def cleared(width, name, eng):
-            t = sbuf([P, width], U8, name)
-            eng.memset(t[:].bitcast(I32), 0)
-            return t
+        def cleared(width, name, engine):
+            zeroed = sbuf([P, width], U8, name)
+            engine.memset(zeroed[:].bitcast(I32), 0)
+            return zeroed
 
         def load_words(dst, src):
             nc.sync.dma_start(dst.bitcast(I32), src[0].bitcast(I32))
 
-        def deal_words(eng, raw, name):
-            t = sbuf([P, 2 * D], U8, name)
-            eng.tensor_copy(
-                t[:].rearrange("p (t m b) -> p t m b", t=PACK, b=2), raw.rearrange("p (m t b) -> p t m b", t=PACK, b=2)
-            )
-            return t
+        def load_gain(src, name):
+            gain = sbuf([P, PACK], F32, name)
+            nc.sync.dma_start(gain[:], src.rearrange("(p t) o -> p (t o)", t=PACK))
+            return gain
 
-        def deal_scales(eng, raw, name, cuts=((0, PACK),)):
-            t = sbuf([P, D], U8, name)
-            for lo, hi in cuts:
-                eng.tensor_copy(
-                    t[:].rearrange("p (t m) -> p t m", t=PACK)[:, lo:hi, :], raw[:].rearrange("p (m t) -> p t m", t=PACK)[:, lo:hi, :]
-                )
-            return t
+        def deal_words(engine, raw, name):
+            dealt = sbuf([P, 2 * D], U8, name)
+            engine.tensor_copy(
+                dealt[:].rearrange("p (t m b) -> p t m b", t=PACK, b=2), raw.rearrange("p (m t b) -> p t m b", t=PACK, b=2)
+            )
+            return dealt
+
+        def deal_scales(engine, raw, name):
+            dealt = sbuf([P, D], U8, name)
+            engine.tensor_copy(dealt[:].rearrange("p (t m) -> p t m", t=PACK), raw[:].rearrange("p (m t) -> p t m", t=PACK))
+            return dealt
 
         def product(out, words, scales, t, codes, code_scales):
             nc.tensor.matmul_mx(
@@ -83,23 +93,25 @@ def tile_picked_forkcrossbsendgap_none_po_kernel(
                 stop=True,
             )
 
+        def turned_sum(dst, first, second):
+            nc.tensor.matmul(dst, first, ident[:], start=True, stop=False, is_transpose=True)
+            nc.tensor.matmul(dst, second, ident[:], start=False, stop=True, is_transpose=True)
+
         def interleave(copy, dst, src):
-            copy(dst[:].rearrange("p (c i t) -> p c t i", i=4, t=PACK), src[:].rearrange("p t (c i) -> p c t i", i=4))
+            copy(dst[:].rearrange("p (c i t) -> p c t i", i=LINE, t=PACK), src[:].rearrange("p t (c i) -> p c t i", i=LINE))
 
         xs = cleared(T, "xs", nc.vector)
         ws_raw = cleared(D, "ws_raw", nc.gpsimd)
         offs_t = load_list(offs, "offs_t")
         w1_raw = sbuf([P, 2 * D], U8, "w1_raw")
         load_words(w1_raw[:], w1_words)
-        gn_t = sbuf([P, PACK], F32, "gn_t")
-        nc.sync.dma_start(gn_t[:], gn.rearrange("(p t) o -> p (t o)", t=PACK))
+        gn_t = load_gain(gn, "gn_t")
         xw = sbuf([P, T], U32, "xw")
         nc.sync.dma_start(xw[:].bitcast(I32), x_words[0].rearrange("p n t -> p (n t)").bitcast(I32))
-        load_scale_rows((nc.scalar,) * 4, ws_raw, w1_scales)
-        load_scale_rows((nc.sync,) * 4, xs, x_scales)
+        load_scale_rows(nc.scalar, ws_raw, w1_scales)
+        load_scale_rows(nc.sync, xs, x_scales)
         n1_t = load_list(n1, "n1_t")
-        gm_t = sbuf([P, PACK], F32, "gm_t")
-        nc.sync.dma_start(gm_t[:], gm.rearrange("(p t) o -> p (t o)", t=PACK))
+        gm_t = load_gain(gm, "gm_t")
         n3_t = load_list(n3, "n3_t")
         n2_t = load_list(n2, "n2_t")
         n4_t = load_list(n4, "n4_t")
@@ -114,35 +126,46 @@ def tile_picked_forkcrossbsendgap_none_po_kernel(
         xq = sbuf([P, S], U32, "xq")
         nc.vector.tensor_copy(xq[:], xw[:].indirect(offs_t[:]))
         xq_s = sbuf([P, S], U8, "xq_s", tag="xw")
-        nc.vector.tensor_copy(xq_s[:], xs[:].indirect(offs_t[:]))
-        y = [bank(f"y{t}", f"acc{t}") for t in range(PACK)]
-        for t in range(PACK):
-            product(y[t][:], w1, w1s, t, xq[:], xq_s[:])
+        halves = [slice(HALF * h, HALF * (h + 1)) for h in range(2)]
+        y0 = [bank(f"y0{h}", f"turned{h}") for h in range(2)]
+        for h in range(2):
+            nc.vector.tensor_copy(xq_s[:, halves[h]], xs[:].indirect(entries(offs_t, HALF * h, HALF)))
+            product(y0[h][:, 0:HALF], w1, w1s, 0, xq[:, halves[h]], xq_s[:, halves[h]])
+        y = [[(halves[h], y0[h][:, 0:HALF]) for h in range(2)]]
+        for t in range(1, PACK):
+            y_bank = bank(f"y{t}", f"acc{t}")
+            product(y_bank[:], w1, w1s, t, xq[:], xq_s[:])
+            y.append([(slice(0, S), y_bank[:])])
+
         w_raw = sbuf([P, 2, 2 * D], U8, "w_raw", tag="xs")
         load_words(w_raw[:, 0, :], w2_words)
         load_words(w_raw[:, 1, :], w3_words)
-        load_scale_rows((nc.sync,) * 4, ws_raw, w2_scales)
+        load_scale_rows(nc.sync, ws_raw, w2_scales)
         w2s = deal_scales(nc.gpsimd, ws_raw, "w2s")
-        load_scale_rows((nc.sync,) * 4, ws_raw, w3_scales)
+        load_scale_rows(nc.sync, ws_raw, w3_scales)
         w2 = deal_words(nc.gpsimd, w_raw[:, 0, :], "w2")
         w3s = deal_scales(nc.gpsimd, ws_raw, "w3s")
         w3 = deal_words(nc.gpsimd, w_raw[:, 1, :], "w3")
 
         sent = [sbuf([P, S], F32, f"sent{t}") for t in range(PACK)]
-        nc.vector.tensor_scalar(sent[0][:], y[0][:], 0.0, gn_t[:, 0:1], ALU.max, ALU.mult)
+        for cols, piece in y[0]:
+            nc.vector.tensor_scalar(sent[0][:, cols], piece, 0.0, gn_t[:, 0:1], ALU.max, ALU.mult)
         for t in range(1, PACK):
             pos = sbuf([P, S], F32, f"pos{t}")
-            nc.scalar.activation(pos[:], y[t][:], ACT.Relu)
+            nc.scalar.activation(pos[:], y[t][0][1], ACT.Relu)
             nc.scalar.activation(sent[t][:], pos[:], ACT.Copy, scale=gn_t[:, t : t + 1])
         ds = [sbuf([P, 2 * S], F32, f"ds{t}") for t in range(PACK)]
         for t in range(PACK):
             nc.vector.tensor_copy(ds[t][:].indirect(n1_t[:]), sent[t][:])
-        less = [sbuf([P, S], F32, f"less{t}") for t in range(PACK)]
+
+        less = [sbuf([P, S], F32, f"less{t}", tag="xw" if t == 0 else None) for t in range(PACK)]
         for t in range(PACK):
-            nc.scalar.activation(less[t][:], y[t][:], ACT.Copy, scale=half_gn[:, t : t + 1])
-        ym = [sbuf([P, S], F32, f"ym{t}") for t in range(PACK)]
+            for cols, piece in y[t]:
+                nc.scalar.activation(less[t][:, cols], piece, ACT.Copy, scale=half_gn[:, t : t + 1])
+        ym = [sbuf([P, S], F32, f"ym{t}", tag="xq" if t == 0 else None) for t in range(PACK)]
         for t in range(PACK):
-            nc.scalar.activation(ym[t][:], y[t][:], ACT.Copy, scale=gm_t[:, t : t + 1])
+            for cols, piece in y[t]:
+                nc.scalar.activation(ym[t][:, cols], piece, ACT.Copy, scale=gm_t[:, t : t + 1])
 
         back = [bank(f"back{h}", f"back{h}") for h in range(2)]
         for u in range(2):
@@ -151,47 +174,46 @@ def tile_picked_forkcrossbsendgap_none_po_kernel(
                 t = 2 * u + e
                 for h in range(2):
                     for c in range(2):
-                        cols = slice(256 * h + P * c, 256 * h + P * (c + 1))
-                        dst = turned[h][:, P * (2 * c + e) : P * (2 * c + e + 1)]
-                        nc.tensor.matmul(dst, less[t][:, cols], ident[:], start=True, stop=False, is_transpose=True)
-                        nc.tensor.matmul(dst, ds[t][:, cols], ident[:], start=False, stop=True, is_transpose=True)
+                        cols = slice(HALF * h + P * c, HALF * h + P * (c + 1))
+                        turned_sum(turned[h][:, P * (2 * c + e) : P * (2 * c + e + 1)], less[t][:, cols], ds[t][:, cols])
             for h in range(2):
-                pairs = sbuf([P, 512], BF16, f"pairs{u}{h}")
+                pairs = sbuf([P, 2 * 2 * P], BF16, f"pairs{u}{h}")
                 nc.scalar.copy(
                     pairs[:].rearrange("j (c p e) -> j c p e", c=2, e=2), turned[h][:].rearrange("j (c e p) -> j c p e", c=2, e=2)
                 )
                 for c in range(2):
                     nc.tensor.transpose(
-                        back[h][:, 256 * u + P * c : 256 * u + P * (c + 1)],
+                        back[h][:, HALF * u + P * c : HALF * u + P * (c + 1)],
                         pairs[:].bitcast(F32)[:, P * c : P * (c + 1)],
                         ident[:],
                     )
         z_in = sbuf([P, PACK * S], BF16, "z_in")
         for h in range(2):
             nc.scalar.copy(
-                z_in[:].bitcast(F32)[:, 512 * h : 512 * (h + 1)].rearrange("p (j u) -> p j u", u=2),
+                z_in[:].bitcast(F32)[:, 2 * HALF * h : 2 * HALF * (h + 1)].rearrange("p (j u) -> p j u", u=2),
                 back[h][:].rearrange("p (u j) -> p j u", u=2),
             )
 
-        def fetch(h, reuse):
-            second = sbuf([P, PACK, 256], F32, f"second{h}", tag=reuse)
+        def fetch_n3(h, tag=None):
+            second = sbuf([P, PACK, HALF], F32, f"second{h}", tag=tag)
             for t in range(PACK):
-                nc.vector.tensor_copy(second[:, t, :], ym[t][:].indirect(n3_t[:, 16 * h : 16 * (h + 1)]))
+                nc.vector.tensor_copy(second[:, t, :], ym[t][:].indirect(entries(n3_t, HALF * h, HALF)))
             return second
 
-        def gap(k, second, reuse=None):
-            c0, w = CHUNKS[k]
-            cut = slice(c0 // 16, (c0 + w) // 16)
-            diff = sbuf([P, PACK, w], F32, f"diff{k}", tag=reuse)
+        def difference(k, second, tag=None):
+            first, width = CHUNKS[k]
+            diff = sbuf([P, PACK, width], F32, f"diff{k}", tag=tag)
             for t in range(PACK):
                 nc.vector.tensor_tensor(
-                    diff[:, t, :], ym[t][:].indirect(n2_t[:, cut]), second[:, t, c0 % 256 : c0 % 256 + w], ALU.subtract
+                    diff[:, t, :],
+                    ym[t][:].indirect(entries(n2_t, first, width)),
+                    second[:, t, first % HALF : first % HALF + width],
+                    ALU.subtract,
                 )
             return diff
 
-        def round_gap(k, diff, reuse=None):
-            w = CHUNKS[k][1]
-            z2_in = sbuf([P, PACK * w], BF16, f"z2_in{k}", tag=reuse)
+        def round_z2(k, diff, tag=None):
+            z2_in = sbuf([P, PACK * CHUNKS[k][1]], BF16, f"z2_in{k}", tag=tag)
             interleave(nc.scalar.copy, z2_in, diff)
             return z2_in
 
@@ -200,76 +222,113 @@ def tile_picked_forkcrossbsendgap_none_po_kernel(
         b = [sbuf([P, S], F32, f"b{t}") for t in range(PACK)]
         b_tags = (("turned0", "turned1"), ("back0",), ("back1",))
 
-        def third(k, z2_in):
-            c0, w = CHUNKS[k]
-            cols = slice(c0, c0 + w)
+        def third_product(k, z2_in):
+            first, width = CHUNKS[k]
+            cols = slice(first, first + width)
             nc.vector.quantize_mx(out=z2_codes[:, cols].bitcast(FP8X4), scales=z2_scales[:, cols], in_=z2_in[:])
             banks = [bank(f"bacc{k}{i}", tag) for i, tag in enumerate(b_tags[k])]
-            per = 512 // w
-            places = [banks[t // per][:, w * (t % per) : w * (t % per + 1)] for t in range(PACK)]
+            per_bank = BANK // width
+            places = [banks[t // per_bank][:, width * (t % per_bank) : width * (t % per_bank + 1)] for t in range(PACK)]
             for t in range(PACK):
                 product(places[t], w3, w3s, t, z2_codes[:, cols], z2_scales[:, cols])
             return places
 
         def drain_b(k, places):
-            c0, w = CHUNKS[k]
+            first, width = CHUNKS[k]
             for t in range(PACK):
-                nc.scalar.copy(b[t][:, c0 : c0 + w], places[t])
+                nc.scalar.copy(b[t][:, first : first + width], places[t])
 
-        diff0 = gap(0, fetch(0, "sent3"))
+        diff0 = difference(0, fetch_n3(0))
         z_codes = sbuf([P, S], U32, "z_codes")
         z_scales = sbuf([P, S], U8, "z_scales")
         nc.vector.quantize_mx(out=z_codes[:].bitcast(FP8X4), scales=z_scales[:], in_=z_in[:])
-        acc = [bank(f"a{t}", f"acc{t}") for t in range(PACK)]
+        a_banks = [bank(f"a_bank{t}", f"acc{t}") for t in range(PACK)]
         for t in range(PACK):
-            product(acc[t][:], w2, w2s, t, z_codes[:], z_scales[:])
-        z2_in0 = round_gap(0, diff0, "pairs11")
+            product(a_banks[t][:], w2, w2s, t, z_codes[:], z_scales[:])
+        z2_in0 = round_z2(0, diff0, "pairs11")
         a = [sbuf([P, S], F32, f"a{t}") for t in range(PACK)]
         for t in range(PACK):
-            nc.scalar.activation(a[t][:], acc[t][:], ACT.Copy, scale=0.75)
-        second1 = fetch(1, "z_in")
-        diff1 = gap(1, second1)
-        places0 = third(0, z2_in0)
-        diff2 = gap(2, second1, "pairs11")
-        z2_in1 = round_gap(1, diff1)
-        drain_b(0, places0)
-        places1 = third(1, z2_in1)
-        z2_in2 = round_gap(2, diff2)
+            nc.scalar.activation(a[t][:], a_banks[t][:], ACT.Copy, scale=0.75)
+        second1 = fetch_n3(1, "z_in")
+        diff1 = difference(1, second1)
+        places0 = third_product(0, z2_in0)
+        diff2 = difference(2, second1, "diff0")
+        z2_in1 = round_z2(1, diff1)
+        b_neg = [sbuf([P, CHUNKS[0][1]], F32, f"b_neg{t}") for t in range(PACK)]
+        for t in range(PACK):
+            nc.scalar.activation(b_neg[t][:], places0[t], ACT.Copy, scale=-1.0)
+        places1 = third_product(1, z2_in1)
+        z2_in2 = round_z2(2, diff2)
         drain_b(1, places1)
+        drain_b(0, places0)
 
-        def cross(c0, w, name, window, plain, offsets):
-            res = sbuf([P, PACK, w], F32, f"{name}{c0}")
+        def cross(k, name, window, plain, held):
+            first, width = CHUNKS[k]
+            crossed = sbuf([P, PACK, width], F32, f"{name}{first}")
             for t in range(PACK):
                 nc.vector.tensor_tensor(
-                    res[:, t, :], window[t][:].indirect(offsets[:, c0 // 16 : (c0 + w) // 16]), plain[t][:, c0 : c0 + w], ALU.mult
+                    crossed[:, t, :], window[t][:].indirect(entries(held, first, width)), plain[t][:, first : first + width], ALU.mult
                 )
-            return res
+            return crossed
 
-        minus = [cross(0, 256, "minus", a, b, n4_t)]
-        places2 = third(2, z2_in2)
+        minus = [cross(0, "minus", a, b_neg, n4_t)]
+        places2 = third_product(2, z2_in2)
         drain_b(2, places2)
-        minus.append(cross(256, 128, "minus", a, b, n4_t))
+        minus.append(cross(1, "minus", a, b, n4_t))
 
         o_codes = sbuf([P, S], U32, "o_codes")
         o_scales = sbuf([P, S], U8, "o_scales")
         rows = out_0.rearrange("(p t) j -> p t j", t=PACK)
         words_out = out_1[0].rearrange("p n t -> p (n t)").bitcast(I32)
-        last = len(CHUNKS) - 1
-        rounded = []
-        for k, (c0, w) in enumerate(CHUNKS):
-            if k == last:
-                minus.append(cross(c0, w, "minus", a, b, n4_t))
-            plus = cross(c0, w, "plus", b, a, n5_t)
-            res = sbuf([P, PACK, w], F32, f"res{k}")
-            nc.vector.tensor_tensor(res[:], plus[:], minus[k][:], ALU.subtract)
-            nc.sync.dma_start(rows[:, :, c0 : c0 + w], res[:])
-            o_in = sbuf([P, PACK * w], BF16, f"o_in{k}")
-            interleave(nc.vector.tensor_copy if k == last else nc.scalar.copy, o_in, res)
-            rounded.append(o_in)
-        for k, (c0, w) in enumerate(CHUNKS):
-            cols = slice(c0, c0 + w)
-            nc.vector.quantize_mx(out=o_codes[:, cols].bitcast(FP8X4), scales=o_scales[:, cols], in_=rounded[k][:])
-            nc.sync.dma_start(words_out[:, cols], o_codes[:, cols].bitcast(I32))
-        for q in range(4):
+
+        plus = cross(0, "plus", b, a, n5_t)
+        summed = [bank(f"summed{c}", f"acc{c}") for c in range(2)]
+        for t in range(PACK):
+            for c in range(2):
+                cols = slice(P * c, P * (c + 1))
+                turned_sum(summed[c][:, P * t : P * (t + 1)], minus[0][:, t, cols], plus[:, t, cols])
+        lying = [sbuf([P, PACK * P], F32, f"lying{c}") for c in range(2)]
+        upright = [bank(f"upright{c}", f"acc{2 + c}") for c in range(2)]
+        for c in range(2):
+            nc.scalar.copy(lying[c][:], summed[c][:])
+            for t in range(PACK):
+                nc.tensor.transpose(upright[c][:, P * t : P * (t + 1)], lying[c][:, P * t : P * (t + 1)], ident[:])
+        o_in0 = sbuf([P, PACK * CHUNKS[0][1]], BF16, "o_in0")
+        for c in range(2):
+            block = sbuf([P, PACK, P], F32, f"res0{c}")
+            nc.scalar.copy(block[:].rearrange("p t j -> p (t j)"), upright[c][:])
+            nc.sync.dma_start(rows[:, :, P * c : P * (c + 1)], block[:])
+            nc.scalar.copy(
+                o_in0[:, PACK * P * c : PACK * P * (c + 1)].rearrange("p (j t) -> p j t", t=PACK),
+                upright[c][:].rearrange("p (t j) -> p j t", t=PACK),
+            )
+
+        def subtract_and_store(k, plus_k, plane_groups):
+            first, width = CHUNKS[k]
+            res = sbuf([P, PACK, width], F32, f"res{k}")
+            for group in plane_groups:
+                nc.vector.tensor_tensor(res[:, group, :], plus_k[:, group, :], minus[k][:, group, :], ALU.subtract)
+            nc.sync.dma_start(rows[:, :, first : first + width], res[:])
+            return res
+
+        def quantise_out(k, o_in):
+            first, width = CHUNKS[k]
+            cols = slice(first, first + width)
+            nc.vector.quantize_mx(out=o_codes[:, cols].bitcast(FP8X4), scales=o_scales[:, cols], in_=o_in[:])
+
+        res1 = subtract_and_store(1, cross(1, "plus", b, a, n5_t), (slice(0, PACK),))
+        o_in1 = sbuf([P, PACK * CHUNKS[1][1]], BF16, "o_in1", tag="lying1")
+        interleave(nc.scalar.copy, o_in1, res1)
+
+        minus.append(cross(2, "minus", a, b, n4_t))
+        res2 = subtract_and_store(2, cross(2, "plus", b, a, n5_t), (slice(0, 2), slice(2, PACK)))
+        quantise_out(0, o_in0)
+        o_in2 = sbuf([P, PACK * CHUNKS[2][1]], BF16, "o_in2", tag="o_in0")
+        interleave(nc.vector.tensor_copy, o_in2, res2)
+        quantise_out(1, o_in1)
+        quantise_out(2, o_in2)
+
+        nc.sync.dma_start(words_out, o_codes[:].bitcast(I32))
+        for q in range(QUADRANTS):
             queue = nc.scalar if q % 2 == 0 else nc.sync
             queue.dma_start(out_2[0, 4 * q : 4 * q + 4, :].bitcast(I32), o_scales[32 * q : 32 * q + 4, :].bitcast(I32))

from contextlib import ExitStack

import concourse.mybir as mybir
from concourse.masks import make_identity

F32 = mybir.dt.float32
BF16 = mybir.dt.bfloat16
I32 = mybir.dt.int32
U32 = mybir.dt.uint32
U16 = mybir.dt.uint16
U8 = mybir.dt.uint8
FP8X4 = mybir.dt.float8_e4m3fn_x4
FP4X4 = mybir.dt.float4_e2m1fn_x4
ALU = mybir.AluOpType
ACT = mybir.ActivationFunctionType

P = 128
T = 2048
S = 512
D = 512
PACK = 4
BANK = 512
HALF = S // 2
GROUP = 16
QUADRANTS = 4
LINE = 4
CHUNKS = ((0, 256), (256, 128), (384, 128))

FLOPS = 3 * 2 * D * D * S


def tile_picked_forkcrossbsendgap_none_po_kernel(
    tc, x_words, x_scales, w1_words, w1_scales, gn, w2_words, w2_scales, gm, w3_words, w3_scales,
    offs, n1, n2, n3, n4, n5, out_0, out_1, out_2,
):
    nc = tc.nc
    with ExitStack() as ctx:
        lists = ctx.enter_context(tc.tile_pool(name="lists", bufs=1))
        sb = ctx.enter_context(tc.tile_pool(name="sb", bufs=1))
        ps = ctx.enter_context(tc.psum_pool(name="ps", bufs=1))

        def sbuf(shape, dtype, name, tag=None):
            return sb.tile(shape, dtype, name=name, tag=tag or name, align_bytes=64)

        def bank(name, tag):
            return ps.tile([P, BANK], F32, name=name, tag=tag)

        def load_list(src, name):
            held = lists.tile([P, S // GROUP], U16, name=name)
            nc.sync.dma_start(held[:], src)
            return held

        def entries(held, first, count):
            return held[:, first // GROUP : (first + count) // GROUP]

        def load_scale_rows(queue, dst, src):
            for q in range(QUADRANTS):
                queue.dma_start(dst[32 * q : 32 * q + 4, :].bitcast(I32), src[0, 4 * q : 4 * q + 4, :].bitcast(I32))

        def cleared(width, name, engine):
            zeroed = sbuf([P, width], U8, name)
            engine.memset(zeroed[:].bitcast(I32), 0)
            return zeroed

        def load_words(dst, src):
            nc.sync.dma_start(dst.bitcast(I32), src[0].bitcast(I32))

        def load_gain(src, name):
            gain = sbuf([P, PACK], F32, name)
            nc.sync.dma_start(gain[:], src.rearrange("(p t) o -> p (t o)", t=PACK))
            return gain

        def deal_words(engine, raw, name):
            dealt = sbuf([P, 2 * D], U8, name)
            engine.tensor_copy(
                dealt[:].rearrange("p (t m b) -> p t m b", t=PACK, b=2), raw.rearrange("p (m t b) -> p t m b", t=PACK, b=2)
            )
            return dealt

        def deal_scales(engine, raw, name):
            dealt = sbuf([P, D], U8, name)
            engine.tensor_copy(dealt[:].rearrange("p (t m) -> p t m", t=PACK), raw[:].rearrange("p (m t) -> p t m", t=PACK))
            return dealt

        def product(out, words, scales, t, codes, code_scales):
            nc.tensor.matmul_mx(
                out=out,
                lhsT=words[:, 2 * P * t : 2 * P * (t + 1)].bitcast(FP4X4),
                lhsT_scale=scales[:, P * t : P * (t + 1)],
                rhs=codes.bitcast(FP8X4),
                rhs_scale=code_scales,
                start=True,
                stop=True,
            )

        def turned_sum(dst, first, second):
            nc.tensor.matmul(dst, first, ident[:], start=True, stop=False, is_transpose=True)
            nc.tensor.matmul(dst, second, ident[:], start=False, stop=True, is_transpose=True)

        def interleave(copy, dst, src):
            copy(dst[:].rearrange("p (c i t) -> p c t i", i=LINE, t=PACK), src[:].rearrange("p t (c i) -> p c t i", i=LINE))

        xs = cleared(T, "xs", nc.vector)
        ws_raw = cleared(D, "ws_raw", nc.gpsimd)
        offs_t = load_list(offs, "offs_t")
        w1_raw = sbuf([P, 2 * D], U8, "w1_raw")
        load_words(w1_raw[:], w1_words)
        gn_t = load_gain(gn, "gn_t")
        xw = sbuf([P, T], U32, "xw")
        nc.sync.dma_start(xw[:].bitcast(I32), x_words[0].rearrange("p n t -> p (n t)").bitcast(I32))
        load_scale_rows(nc.scalar, ws_raw, w1_scales)
        load_scale_rows(nc.sync, xs, x_scales)
        n1_t = load_list(n1, "n1_t")
        gm_t = load_gain(gm, "gm_t")
        n3_t = load_list(n3, "n3_t")
        n2_t = load_list(n2, "n2_t")
        n4_t = load_list(n4, "n4_t")
        n5_t = load_list(n5, "n5_t")
        ident = sbuf([P, P], F32, "ident")
        make_identity(nc, ident[:])
        half_gn = sbuf([P, PACK], F32, "half_gn")
        nc.scalar.activation(half_gn[:], gn_t[:], ACT.Copy, scale=-0.5)

        w1 = deal_words(nc.vector, w1_raw[:], "w1")
        w1s = deal_scales(nc.vector, ws_raw, "w1s")
        xq = sbuf([P, S], U32, "xq")
        nc.vector.tensor_copy(xq[:], xw[:].indirect(offs_t[:]))
        xq_s = sbuf([P, S], U8, "xq_s", tag="xw")
        halves = [slice(HALF * h, HALF * (h + 1)) for h in range(2)]
        y0 = [bank(f"y0{h}", f"turned{h}") for h in range(2)]
        for h in range(2):
            nc.vector.tensor_copy(xq_s[:, halves[h]], xs[:].indirect(entries(offs_t, HALF * h, HALF)))
            product(y0[h][:, 0:HALF], w1, w1s, 0, xq[:, halves[h]], xq_s[:, halves[h]])
        y = [[(halves[h], y0[h][:, 0:HALF]) for h in range(2)]]
        for t in range(1, PACK):
            y_bank = bank(f"y{t}", f"acc{t}")
            product(y_bank[:], w1, w1s, t, xq[:], xq_s[:])
            y.append([(slice(0, S), y_bank[:])])

        w_raw = sbuf([P, 2, 2 * D], U8, "w_raw", tag="xs")
        load_words(w_raw[:, 0, :], w2_words)
        load_words(w_raw[:, 1, :], w3_words)
        load_scale_rows(nc.sync, ws_raw, w2_scales)
        w2s = deal_scales(nc.gpsimd, ws_raw, "w2s")
        load_scale_rows(nc.sync, ws_raw, w3_scales)
        w2 = deal_words(nc.gpsimd, w_raw[:, 0, :], "w2")
        w3s = deal_scales(nc.gpsimd, ws_raw, "w3s")
        w3 = deal_words(nc.gpsimd, w_raw[:, 1, :], "w3")

        sent = [sbuf([P, S], F32, f"sent{t}") for t in range(PACK)]
        for cols, piece in y[0]:
            nc.vector.tensor_scalar(sent[0][:, cols], piece, 0.0, gn_t[:, 0:1], ALU.max, ALU.mult)
        for t in range(1, PACK):
            pos = sbuf([P, S], F32, f"pos{t}")
            nc.scalar.activation(pos[:], y[t][0][1], ACT.Relu)
            nc.scalar.activation(sent[t][:], pos[:], ACT.Copy, scale=gn_t[:, t : t + 1])
        ds = [sbuf([P, 2 * S], F32, f"ds{t}") for t in range(PACK)]
        for t in range(PACK):
            nc.vector.tensor_copy(ds[t][:].indirect(n1_t[:]), sent[t][:])

        less = [sbuf([P, S], F32, f"less{t}", tag="xw" if t == 0 else None) for t in range(PACK)]
        for t in range(PACK):
            for cols, piece in y[t]:
                nc.scalar.activation(less[t][:, cols], piece, ACT.Copy, scale=half_gn[:, t : t + 1])
        ym = [sbuf([P, S], F32, f"ym{t}", tag="xq" if t == 0 else None) for t in range(PACK)]
        for t in range(PACK):
            for cols, piece in y[t]:
                nc.scalar.activation(ym[t][:, cols], piece, ACT.Copy, scale=gm_t[:, t : t + 1])

        back = [bank(f"back{h}", f"back{h}") for h in range(2)]
        for u in range(2):
            turned = [bank(f"turned{u}{h}", f"turned{h}") for h in range(2)]
            for e in range(2):
                t = 2 * u + e
                for h in range(2):
                    for c in range(2):
                        cols = slice(HALF * h + P * c, HALF * h + P * (c + 1))
                        turned_sum(turned[h][:, P * (2 * c + e) : P * (2 * c + e + 1)], less[t][:, cols], ds[t][:, cols])
            for h in range(2):
                pairs = sbuf([P, 2 * 2 * P], BF16, f"pairs{u}{h}")
                nc.scalar.copy(
                    pairs[:].rearrange("j (c p e) -> j c p e", c=2, e=2), turned[h][:].rearrange("j (c e p) -> j c p e", c=2, e=2)
                )
                for c in range(2):
                    nc.tensor.transpose(
                        back[h][:, HALF * u + P * c : HALF * u + P * (c + 1)],
                        pairs[:].bitcast(F32)[:, P * c : P * (c + 1)],
                        ident[:],
                    )
        z_in = sbuf([P, PACK * S], BF16, "z_in")
        for h in range(2):
            nc.scalar.copy(
                z_in[:].bitcast(F32)[:, 2 * HALF * h : 2 * HALF * (h + 1)].rearrange("p (j u) -> p j u", u=2),
                back[h][:].rearrange("p (u j) -> p j u", u=2),
            )

        def fetch_n3(h, tag=None):
            second = sbuf([P, PACK, HALF], F32, f"second{h}", tag=tag)
            for t in range(PACK):
                nc.vector.tensor_copy(second[:, t, :], ym[t][:].indirect(entries(n3_t, HALF * h, HALF)))
            return second

        def difference(k, second, tag=None):
            first, width = CHUNKS[k]
            diff = sbuf([P, PACK, width], F32, f"diff{k}", tag=tag)
            for t in range(PACK):
                nc.vector.tensor_tensor(
                    diff[:, t, :],
                    ym[t][:].indirect(entries(n2_t, first, width)),
                    second[:, t, first % HALF : first % HALF + width],
                    ALU.subtract,
                )
            return diff

        def round_z2(k, diff, tag=None):
            z2_in = sbuf([P, PACK * CHUNKS[k][1]], BF16, f"z2_in{k}", tag=tag)
            interleave(nc.scalar.copy, z2_in, diff)
            return z2_in

        z2_codes = sbuf([P, S], U32, "z2_codes")
        z2_scales = sbuf([P, S], U8, "z2_scales")
        b = [sbuf([P, S], F32, f"b{t}") for t in range(PACK)]
        b_tags = (("turned0", "turned1"), ("back0",), ("back1",))

        def third_product(k, z2_in):
            first, width = CHUNKS[k]
            cols = slice(first, first + width)
            nc.vector.quantize_mx(out=z2_codes[:, cols].bitcast(FP8X4), scales=z2_scales[:, cols], in_=z2_in[:])
            banks = [bank(f"bacc{k}{i}", tag) for i, tag in enumerate(b_tags[k])]
            per_bank = BANK // width
            places = [banks[t // per_bank][:, width * (t % per_bank) : width * (t % per_bank + 1)] for t in range(PACK)]
            for t in range(PACK):
                product(places[t], w3, w3s, t, z2_codes[:, cols], z2_scales[:, cols])
            return places

        def drain_b(k, places):
            first, width = CHUNKS[k]
            for t in range(PACK):
                nc.scalar.copy(b[t][:, first : first + width], places[t])

        diff0 = difference(0, fetch_n3(0))
        z_codes = sbuf([P, S], U32, "z_codes")
        z_scales = sbuf([P, S], U8, "z_scales")
        nc.vector.quantize_mx(out=z_codes[:].bitcast(FP8X4), scales=z_scales[:], in_=z_in[:])
        a_banks = [bank(f"a_bank{t}", f"acc{t}") for t in range(PACK)]
        for t in range(PACK):
            product(a_banks[t][:], w2, w2s, t, z_codes[:], z_scales[:])
        z2_in0 = round_z2(0, diff0, "pairs11")
        a = [sbuf([P, S], F32, f"a{t}") for t in range(PACK)]
        for t in range(PACK):
            nc.scalar.activation(a[t][:], a_banks[t][:], ACT.Copy, scale=0.75)
        second1 = fetch_n3(1, "z_in")
        diff1 = difference(1, second1)
        places0 = third_product(0, z2_in0)
        diff2 = difference(2, second1, "diff0")
        z2_in1 = round_z2(1, diff1)
        b_neg = [sbuf([P, CHUNKS[0][1]], F32, f"b_neg{t}") for t in range(PACK)]
        for t in range(PACK):
            nc.scalar.activation(b_neg[t][:], places0[t], ACT.Copy, scale=-1.0)
        places1 = third_product(1, z2_in1)
        z2_in2 = round_z2(2, diff2)
        drain_b(1, places1)
        drain_b(0, places0)

        def cross(k, name, window, plain, held):
            first, width = CHUNKS[k]
            crossed = sbuf([P, PACK, width], F32, f"{name}{first}")
            for t in range(PACK):
                nc.vector.tensor_tensor(
                    crossed[:, t, :], window[t][:].indirect(entries(held, first, width)), plain[t][:, first : first + width], ALU.mult
                )
            return crossed

        minus = [cross(0, "minus", a, b_neg, n4_t)]
        places2 = third_product(2, z2_in2)
        drain_b(2, places2)
        minus.append(cross(1, "minus", a, b, n4_t))

        o_codes = sbuf([P, S], U32, "o_codes")
        o_scales = sbuf([P, S], U8, "o_scales")
        rows = out_0.rearrange("(p t) j -> p t j", t=PACK)
        words_out = out_1[0].rearrange("p n t -> p (n t)").bitcast(I32)

        plus = cross(0, "plus", b, a, n5_t)
        summed = [bank(f"summed{c}", f"acc{c}") for c in range(2)]
        for t in range(PACK):
            for c in range(2):
                cols = slice(P * c, P * (c + 1))
                turned_sum(summed[c][:, P * t : P * (t + 1)], minus[0][:, t, cols], plus[:, t, cols])
        lying = [sbuf([P, PACK * P], F32, f"lying{c}") for c in range(2)]
        upright = [bank(f"upright{c}", f"acc{2 + c}") for c in range(2)]
        for c in range(2):
            nc.scalar.copy(lying[c][:], summed[c][:])
            for t in range(PACK):
                nc.tensor.transpose(upright[c][:, P * t : P * (t + 1)], lying[c][:, P * t : P * (t + 1)], ident[:])
        o_in0 = sbuf([P, PACK * CHUNKS[0][1]], BF16, "o_in0")
        for c in range(2):
            block = sbuf([P, PACK, P], F32, f"res0{c}")
            nc.scalar.copy(block[:].rearrange("p t j -> p (t j)"), upright[c][:])
            nc.sync.dma_start(rows[:, :, P * c : P * (c + 1)], block[:])
            nc.scalar.copy(
                o_in0[:, PACK * P * c : PACK * P * (c + 1)].rearrange("p (j t) -> p j t", t=PACK),
                upright[c][:].rearrange("p (t j) -> p j t", t=PACK),
            )

        def subtract_and_store(k, plus_k, plane_groups):
            first, width = CHUNKS[k]
            res = sbuf([P, PACK, width], F32, f"res{k}")
            for group in plane_groups:
                nc.vector.tensor_tensor(res[:, group, :], plus_k[:, group, :], minus[k][:, group, :], ALU.subtract)
            nc.sync.dma_start(rows[:, :, first : first + width], res[:])
            return res

        def quantise_out(k, o_in):
            first, width = CHUNKS[k]
            cols = slice(first, first + width)
            nc.vector.quantize_mx(out=o_codes[:, cols].bitcast(FP8X4), scales=o_scales[:, cols], in_=o_in[:])

        res1 = subtract_and_store(1, cross(1, "plus", b, a, n5_t), (slice(0, PACK),))
        o_in1 = sbuf([P, PACK * CHUNKS[1][1]], BF16, "o_in1", tag="lying1")
        interleave(nc.scalar.copy, o_in1, res1)

        minus.append(cross(2, "minus", a, b, n4_t))
        res2 = subtract_and_store(2, cross(2, "plus", b, a, n5_t), (slice(0, 2), slice(2, PACK)))
        quantise_out(0, o_in0)
        o_in2 = sbuf([P, PACK * CHUNKS[2][1]], BF16, "o_in2", tag="o_in0")
        interleave(nc.vector.tensor_copy, o_in2, res2)
        quantise_out(1, o_in1)
        quantise_out(2, o_in2)

        nc.sync.dma_start(words_out, o_codes[:].bitcast(I32))
        for q in range(QUADRANTS):
            queue = nc.scalar if q % 2 == 0 else nc.sync
            queue.dma_start(out_2[0, 4 * q : 4 * q + 4, :].bitcast(I32), o_scales[32 * q : 32 * q + 4, :].bitcast(I32))
